import numpy as np
import ml_dtypes


def mxq(x, axis, fmt="e4m3"):
    dtype, down = {"e4m3": (ml_dtypes.float8_e4m3fn, 7), "e5m2": (ml_dtypes.float8_e5m2, 14)}[fmt]
    v = np.moveaxis(np.asarray(x, np.float32).astype(ml_dtypes.bfloat16).astype(np.float64), axis, -1)
    blocks = v.reshape(v.shape[:-1] + (-1, 32))
    amax = np.abs(blocks).max(-1, keepdims=True)
    byte = np.maximum(np.where(amax > 0, np.frexp(amax)[1] - 1 + 127, 0) - down, 1)
    scale = np.exp2(byte - 127.0)
    codes = (blocks / scale).astype(np.float32).astype(dtype).astype(np.float64)
    return np.moveaxis((codes * scale).reshape(v.shape), -1, axis)


WIDE = False


def mx_kscale(k):
    if not WIDE:
        return np.ones(k)
    levels = np.array([10, -10, 5, -5, 0])
    if k % 512:
        return np.exp2(np.random.permutation(np.resize(levels, k // 32))).repeat(32)
    a = np.empty((k // 512, 16))
    for p in range(k // 512):
        a[p, :8] = np.random.permutation(np.resize(levels, 8))
        for g in range(8):
            far = levels[np.abs(levels - a[p, g]) >= 10]
            a[p, g + 8] = far[np.random.randint(len(far))]
    return np.exp2(a.ravel()).repeat(32)


def f64(x):
    return np.asarray(x).astype(np.float64)


E2M1 = np.array([0.0, 0.5, 1.0, 1.5, 2.0, 3.0, 4.0, 6.0, -0.0, -0.5, -1.0, -1.5, -2.0, -3.0, -4.0, -6.0])


def pack_weight(w, fmt):
    k, n = w.shape
    w = f64(np.asarray(w, np.float32).astype(ml_dtypes.bfloat16)).reshape(k // 32, 32, n)
    amax = np.abs(w).max(1)
    if fmt == "e4m3":
        byte = np.frexp(amax)[1] - 1 + 127 - 7
    else:
        mant, ex = np.frexp(amax / 6.0)
        byte = np.where(mant > 0.5, ex, ex - 1) + 127
    byte = np.clip(np.where(amax > 0, byte, 1), 1, 254)
    scaled = (w * np.exp2(127.0 - byte)[:, None, :]).reshape(k, n).astype(np.float32)
    by_word = np.ascontiguousarray(scaled.reshape(k // 512, 128, 4, n).transpose(0, 1, 3, 2))
    if fmt == "e4m3":
        words = by_word.astype(ml_dtypes.float8_e4m3fn).view(np.uint8)
    else:
        c = by_word.astype(ml_dtypes.float4_e2m1fn).view(np.uint8) & 0xF
        words = (c[..., 0::2] | (c[..., 1::2] << 4)).reshape(k // 512, 128, 2 * n)
    return np.ascontiguousarray(words), np.ascontiguousarray(byte.astype(np.uint8).reshape(k // 512, 16, n))


def unpack_weight(words, scales, fmt):
    g, _, n = scales.shape
    words = np.ascontiguousarray(words).reshape(g, 128, n, -1)
    if fmt == "e4m3":
        vals = words.view(ml_dtypes.float8_e4m3fn).astype(np.float64)
    else:
        nib = np.empty((g, 128, n, 4), np.uint8)
        nib[..., 0::2] = words & 0xF
        nib[..., 1::2] = words >> 4
        vals = E2M1[nib]
    vals = vals * np.repeat(np.exp2(scales.astype(np.float64) - 127.0), 8, axis=1)[..., None]
    return vals.transpose(0, 1, 3, 2).reshape(g * 512, n)


def planes(y):
    n, m = y.shape
    v = y.astype(np.float32).astype(ml_dtypes.bfloat16).astype(np.float64).reshape(n // 32, 32, m)
    top = np.abs(v).max(1)
    byte = np.clip(np.where(top > 0, np.frexp(top)[1] - 1 + 127 - 7, 1), 1, 254)
    codes = (v * np.exp2(127.0 - byte)[:, None, :]).reshape(n, m).astype(np.float32).astype(ml_dtypes.float8_e4m3fn).view(np.uint8)
    words = codes.reshape(n // 512, 128, 4, m).transpose(0, 1, 3, 2)
    return np.ascontiguousarray(words), np.ascontiguousarray(byte.astype(np.uint8).reshape(n // 512, 16, m))


def gelu(v):
    return 0.5 * v * (1.0 + np.tanh(np.sqrt(2.0 / np.pi) * (v + 0.044715 * v**3)))


O, K, M, T = 1024, 2048, 1536, 512


def setup_inputs():
    n = np.random.standard_normal
    s = mx_kscale(K)[:, None]
    x = n((K, T)); x[:O] *= 6.0
    w = n((K, M)) / np.sqrt(K) / s; w[:O] /= 2.0
    p_x4 = pack_weight(x[O:] * s[O:], "e2m1")
    p_w4 = pack_weight(w[O:], "e2m1")
    return {
        "x8": (x[:O] * s[:O]).astype(np.float32),
        "w8": (w[:O]).astype(np.float32),
        "x4_words": p_x4[0],
        "x4_scales": p_x4[1],
        "w4_words": p_w4[0],
        "w4_scales": p_w4[1],
        "b": (0.3 * n(1536)).astype(np.float32),
    }


def reference(x8, w8, x4_words, x4_scales, w4_words, w4_scales, b):
    x8_ = mxq(f64(x8), 0, "e4m3")
    w8_ = mxq(f64(w8), 0, "e4m3")
    x4_ = unpack_weight(x4_words, x4_scales, "e2m1")
    w4_ = unpack_weight(w4_words, w4_scales, "e2m1")
    y = w8_.T @ x8_ + w4_.T @ x4_
    out_0 = gelu(y + f64(b)[:, None])
    return (out_0,) + planes(out_0)

@@ -1,0 +1,233 @@
+from contextlib import ExitStack
+
+import concourse.mybir as mybir
+
+O, M, T = 1024, 1536, 512
+FLOPS = 2 * 2 * O * M * T
+
+F32 = mybir.dt.float32
+BF16 = mybir.dt.bfloat16
+I32 = mybir.dt.int32
+U32 = mybir.dt.uint32
+U8 = mybir.dt.uint8
+FP8X4 = mybir.dt.float8_e4m3fn_x4
+FP4X4 = mybir.dt.float4_e2m1fn_x4
+GELU = mybir.ActivationFunctionType.Gelu_apprx_tanh
+
+P = 128
+PACK = 4
+SPAN = P * PACK
+PASSES = O // SPAN
+GROUPS = M // SPAN
+QUADS = 4
+
+
+def tile_mix_atom_fm_pl_gelu_kernel(
+    tc, x8, w8, x4_words, x4_scales, w4_words, w4_scales, b, out_0, out_1, out_2
+):
+    nc = tc.nc
+    with ExitStack() as ctx:
+        sb = ctx.enter_context(tc.tile_pool(name="sb", bufs=1))
+        psum = ctx.enter_context(tc.psum_pool(name="psum", bufs=2))
+        ctx.enter_context(tc.manual_schedule())
+
+        def tile(name, shape, dtype):
+            return sb.tile(shape, dtype, name=name, align_bytes=64)
+
+        ga = [(g, a) for a in range(GROUPS) for g in range(PASSES)]
+        x_raw = [tile(f"x_raw{g}", [P, PACK, T], F32) for g in range(PASSES)]
+        x_bf = [tile(f"x_bf{g}", [P, T, PACK], BF16) for g in range(PASSES)]
+        x_codes = [tile(f"x_codes{g}", [P, T], U32) for g in range(PASSES)]
+        x_scales = [tile(f"x_scales{g}", [P, T], U8) for g in range(PASSES)]
+        w_raw = {k: tile(f"w_raw{k[0]}{k[1]}", [P, PACK, SPAN], F32) for k in ga}
+        w_bf = {k: tile(f"w_bf{k[0]}{k[1]}", [P, PACK, P, PACK], BF16) for k in ga}
+        w_codes = {k: tile(f"w_codes{k[0]}{k[1]}", [P, SPAN], U32) for k in ga}
+        w_scales = {k: tile(f"w_scales{k[0]}{k[1]}", [P, SPAN], U8) for k in ga}
+        w4_raw = [tile(f"w4_raw{g}", [P, 2 * M], U8) for g in range(PASSES)]
+        w4_dealt = [tile(f"w4_dealt{g}", [P, PACK, 2 * M // PACK], U8) for g in range(PASSES)]
+        x4_codes = tile("x4_codes", [P, PASSES, 2 * T], U8)
+        scale_rows = tile("scale_rows", [P, PASSES, M + T], U8)
+        w4_scales_dealt = tile("w4_scales_dealt", [P, PASSES, PACK, M // PACK], U8)
+        bias = tile("bias", [P, GROUPS, PACK], F32)
+        warm = tile("warm", [P, 2], F32)
+        res = [tile(f"res{a}", [P, PACK, T], F32) for a in range(GROUPS)]
+        res_bf = [tile(f"res_bf{a}", [P, T, PACK], BF16) for a in range(GROUPS)]
+        res_codes = [tile(f"res_codes{a}", [P, T], U32) for a in range(GROUPS)]
+        res_scales = tile("res_scales", [P, GROUPS, T], U8)
+        acc = {}
+
+        def copy_on(engine, out, in_):
+            if engine == "vector":
+                nc.vector.tensor_copy(out=out, in_=in_)
+            else:
+                nc.scalar.copy(out=out, in_=in_)
+
+        def interleave(engine, dst, src, lo, hi):
+            copy_on(
+                engine,
+                dst[:, lo:hi, :].rearrange("p (c i) j -> p c j i", i=4),
+                src[:, :, lo:hi].rearrange("p j (c i) -> p c j i", i=4),
+            )
+
+        def deal_w8(engine, k, lo, hi):
+            copy_on(
+                engine,
+                w_bf[k][:, :, lo:hi, :].rearrange("p r m j -> p m j r"),
+                w_raw[k][:, :, PACK * lo : PACK * hi].rearrange("p j (m r) -> p m j r", r=PACK),
+            )
+
+        def quantize(codes, scales, values):
+            nc.vector.quantize_mx(out=codes.bitcast(FP8X4), scales=scales, in_=values)
+
+        def quantize_x(g):
+            quantize(x_codes[g][:], x_scales[g][:], x_bf[g][:].rearrange("p t j -> p (t j)"))
+
+        def quantize_w(k):
+            quantize(w_codes[k][:], w_scales[k][:], w_bf[k][:].rearrange("p r m j -> p (r m j)"))
+
+        def quantize_w_slot(k, r):
+            cols = slice(r * P, (r + 1) * P)
+            quantize(w_codes[k][:, cols], w_scales[k][:, cols], w_bf[k][:, r, :, :].rearrange("p m j -> p (m j)"))
+
+        def quantize_res(a):
+            quantize(res_codes[a][:], res_scales[:, a, :], res_bf[a][:].rearrange("p t r -> p (t r)"))
+
+        def deal_w4(g):
+            nc.vector.tensor_copy(
+                out=w4_dealt[g][:].rearrange("p r (m e) -> p r m e", e=2),
+                in_=w4_raw[g][:].rearrange("p (m r e) -> p r m e", r=PACK, e=2),
+            )
+
+        def load_w8(k):
+            g, a = k
+            rows = w8[g * SPAN : (g + 1) * SPAN, a * SPAN : (a + 1) * SPAN]
+            nc.sync.dma_start(out=w_raw[k][:], in_=rows.rearrange("(p j) n -> p j n", j=PACK))
+
+        def fp4_passes(a, g):
+            for r in range(PACK):
+                if g == 0:
+                    acc[a, r] = psum.tile([P, T], F32, name=f"acc{r}")
+                nc.tensor.matmul_mx(
+                    out=acc[a, r][:],
+                    lhsT=w4_dealt[g][:, r, 2 * P * a : 2 * P * (a + 1)].bitcast(FP4X4),
+                    lhsT_scale=w4_scales_dealt[:, g, r, P * a : P * (a + 1)],
+                    rhs=x4_codes[:, g, :].bitcast(FP4X4),
+                    rhs_scale=scale_rows[:, g, M:],
+                    start=(g == 0),
+                    stop=False,
+                )
+
+        def fp8_passes(a, g):
+            for r in range(PACK):
+                cols = slice(r * P, (r + 1) * P)
+                nc.tensor.matmul_mx(
+                    out=acc[a, r][:],
+                    lhsT=w_codes[g, a][:, cols].bitcast(FP8X4),
+                    lhsT_scale=w_scales[g, a][:, cols],
+                    rhs=x_codes[g][:].bitcast(FP8X4),
+                    rhs_scale=x_scales[g][:],
+                    start=False,
+                    stop=(g == PASSES - 1),
+                )
+
+        def gelu(a, r, lo, hi):
+            nc.scalar.activation(
+                out=res[a][:, r, lo:hi], in_=acc[a, r][:, lo:hi], func=GELU, bias=bias[:, a, r : r + 1]
+            )
+
+        def store_res(a, lo, hi):
+            rows = out_0[a * SPAN : (a + 1) * SPAN, :].rearrange("(p r) t -> p r t", r=PACK)
+            nc.sync.dma_start(out=rows[:, lo:hi, :], in_=res[a][:, lo:hi, :])
+
+        def store_codes(a):
+            nc.sync.dma_start(
+                out=out_1[a].rearrange("p t i -> p (t i)").bitcast(I32), in_=res_codes[a][:].bitcast(I32)
+            )
+
+        def load_scale_rows(lo, hi, source):
+            for r in range(4):
+                nc.sync.dma_start(
+                    out=scale_rows[r:P:32, :, lo:hi].bitcast(I32),
+                    in_=source[:, r:16:4, :].rearrange("g q n -> q g n").bitcast(I32),
+                )
+
+        def load_x8(g):
+            nc.sync.dma_start(
+                out=x_raw[g][:], in_=x8[g * SPAN : (g + 1) * SPAN, :].rearrange("(p j) t -> p j t", j=PACK)
+            )
+
+        def load_w4(g):
+            nc.sync.dma_start(out=w4_raw[g][:].bitcast(I32), in_=w4_words[g].bitcast(I32))
+
+        nc.vector.memset(scale_rows[:].rearrange("p g n -> p (g n)").bitcast(I32), 0)
+        nc.gpsimd.memset(warm[:, 0:1], 0.0)
+        nc.gpsimd.dma_start(out=bias[:], in_=b.rearrange("(a p r) -> p a r", p=P, r=PACK))
+        nc.scalar.activation(out=warm[:, 1:2], in_=warm[:, 0:1], func=GELU)
+        load_w4(0)
+        load_x8(0)
+        load_scale_rows(0, M, w4_scales)
+        load_w4(1)
+        load_x8(1)
+        load_w8(ga[0])
+        nc.sync.dma_start(
+            out=x4_codes[:].bitcast(I32), in_=x4_words.rearrange("g p n -> p g n").bitcast(I32)
+        )
+        load_scale_rows(M, M + T, x4_scales)
+        for k in ga[1:]:
+            load_w8(k)
+
+        deal_w4(0)
+        interleave("scalar", x_bf[0], x_raw[0], 0, T)
+        nc.vector.tensor_copy(
+            out=w4_scales_dealt[:],
+            in_=scale_rows[:, :, :M].rearrange("p g (m r) -> p g r m", r=PACK),
+        )
+        deal_w4(1)
+        quantize_x(0)
+        interleave("vector", x_bf[1], x_raw[1], 0, 320)
+        interleave("scalar", x_bf[1], x_raw[1], 320, T)
+        quantize_x(1)
+        deal_w8("vector", (0, 0), 0, 80)
+        deal_w8("scalar", (0, 0), 80, P)
+        quantize_w((0, 0))
+        fp4_passes(0, 0)
+        fp4_passes(0, 1)
+        fp8_passes(0, 0)
+
+        for a in range(GROUPS):
+            last = a == GROUPS - 1
+            deal_w8("vector", (1, a), 0, 88)
+            deal_w8("scalar", (1, a), 88, P)
+            for r in range(PACK):
+                quantize_w_slot((1, a), r)
+            fp8_passes(a, 1)
+            if a > 0:
+                interleave("scalar", res_bf[a - 1], res[a - 1], 320, T)
+                interleave("vector", res_bf[a - 1], res[a - 1], 0, 320)
+                quantize_res(a - 1)
+                store_codes(a - 1)
+            if not last:
+                for r in range(PACK):
+                    gelu(a, r, 0, T)
+                store_res(a, 0, PACK)
+                deal_w8("vector", (0, a + 1), 0, P)
+                quantize_w((0, a + 1))
+                fp4_passes(a + 1, 0)
+                fp4_passes(a + 1, 1)
+                fp8_passes(a + 1, 0)
+            else:
+                gelu(a, 0, 0, T)
+                gelu(a, 1, 0, T)
+                store_res(a, 0, 2)
+                for lo, hi in ((0, T // 2), (T // 2, T)):
+                    gelu(a, 2, lo, hi)
+                    gelu(a, 3, lo, hi)
+                    interleave("vector", res_bf[a], res[a], lo, hi)
+                store_res(a, 2, PACK)
+                quantize_res(a)
+                store_codes(a)
+        for q in range(QUADS):
+            nc.scalar.dma_start(
+                out=out_2[:, 4 * q : 4 * q + 4, :].rearrange("a r t -> r a t").bitcast(I32),
+                in_=res_scales[32 * q : 32 * q + 4, :, :].bitcast(I32),
+            )

@@ -46,7 +46,9 @@ def tile_mix_atom_fm_pl_gelu_kernel(
         w4_raw = [tile(f"w4_raw{g}", [P, 2 * M], U8) for g in range(PASSES)]
         w4_dealt = [tile(f"w4_dealt{g}", [P, PACK, 2 * M // PACK], U8) for g in range(PASSES)]
         x4_codes = tile("x4_codes", [P, PASSES, 2 * T], U8)
-        scale_rows = tile("scale_rows", [P, PASSES, M + T], U8)
+        scale_rows = tile("scale_rows", [P, PASSES * (M + T)], U8)
+        w4_scale_rows = scale_rows[:, : PASSES * M].rearrange("p (g n) -> p g n", g=PASSES)
+        x4_scale_rows = scale_rows[:, PASSES * M :].rearrange("p (g t) -> p g t", g=PASSES)
         w4_scales_dealt = tile("w4_scales_dealt", [P, PASSES, PACK, M // PACK], U8)
         bias = tile("bias", [P, GROUPS, PACK], F32)
         warm = tile("warm", [P, 2], F32)
@@ -72,8 +74,8 @@ def tile_mix_atom_fm_pl_gelu_kernel(
         def deal_w8(engine, k, lo, hi):
             copy_on(
                 engine,
-                w_bf[k][:, :, lo:hi, :].rearrange("p r m j -> p m j r"),
-                w_raw[k][:, :, PACK * lo : PACK * hi].rearrange("p j (m r) -> p m j r", r=PACK),
+                w_bf[k][:, :, lo:hi, :].rearrange("p r m j -> p m r j"),
+                w_raw[k][:, :, PACK * lo : PACK * hi].rearrange("p j (m r) -> p m r j", r=PACK),
             )
 
         def quantize(codes, scales, values):
@@ -112,7 +114,7 @@ def tile_mix_atom_fm_pl_gelu_kernel(
                     lhsT=w4_dealt[g][:, r, 2 * P * a : 2 * P * (a + 1)].bitcast(FP4X4),
                     lhsT_scale=w4_scales_dealt[:, g, r, P * a : P * (a + 1)],
                     rhs=x4_codes[:, g, :].bitcast(FP4X4),
-                    rhs_scale=scale_rows[:, g, M:],
+                    rhs_scale=x4_scale_rows[:, g, :],
                     start=(g == 0),
                     stop=False,
                 )
@@ -144,10 +146,10 @@ def tile_mix_atom_fm_pl_gelu_kernel(
                 out=out_1[a].rearrange("p t i -> p (t i)").bitcast(I32), in_=res_codes[a][:].bitcast(I32)
             )
 
-        def load_scale_rows(lo, hi, source):
+        def load_scale_rows(queue, plane, source):
             for r in range(4):
-                nc.sync.dma_start(
-                    out=scale_rows[r:P:32, :, lo:hi].bitcast(I32),
+                queue.dma_start(
+                    out=plane[r:P:32, :, :].bitcast(I32),
                     in_=source[:, r:16:4, :].rearrange("g q n -> q g n").bitcast(I32),
                 )
 
@@ -156,23 +158,39 @@ def tile_mix_atom_fm_pl_gelu_kernel(
                 out=x_raw[g][:], in_=x8[g * SPAN : (g + 1) * SPAN, :].rearrange("(p j) t -> p j t", j=PACK)
             )
 
+        def split_w8(k, cut):
+            deal_w8("vector", k, 0, cut)
+            if cut < P:
+                deal_w8("scalar", k, cut, P)
+
+        def finish_group(a, cut):
+            split_w8((1, a), cut)
+            for r in range(PACK):
+                quantize_w_slot((1, a), r)
+            fp8_passes(a, 1)
+
+        def open_group(a):
+            fp4_passes(a, 0)
+            fp4_passes(a, 1)
+            fp8_passes(a, 0)
+
         def load_w4(g):
             nc.sync.dma_start(out=w4_raw[g][:].bitcast(I32), in_=w4_words[g].bitcast(I32))
 
-        nc.vector.memset(scale_rows[:].rearrange("p g n -> p (g n)").bitcast(I32), 0)
+        nc.vector.memset(scale_rows[:].bitcast(I32), 0)
         nc.gpsimd.memset(warm[:, 0:1], 0.0)
         nc.gpsimd.dma_start(out=bias[:], in_=b.rearrange("(a p r) -> p a r", p=P, r=PACK))
         nc.scalar.activation(out=warm[:, 1:2], in_=warm[:, 0:1], func=GELU)
         load_w4(0)
         load_x8(0)
-        load_scale_rows(0, M, w4_scales)
+        load_scale_rows(nc.sync, w4_scale_rows, w4_scales)
         load_w4(1)
         load_x8(1)
         load_w8(ga[0])
         nc.sync.dma_start(
             out=x4_codes[:].bitcast(I32), in_=x4_words.rearrange("g p n -> p g n").bitcast(I32)
         )
-        load_scale_rows(M, M + T, x4_scales)
+        load_scale_rows(nc.sync, x4_scale_rows, x4_scales)
         for k in ga[1:]:
             load_w8(k)
 
@@ -180,52 +198,52 @@ def tile_mix_atom_fm_pl_gelu_kernel(
         interleave("scalar", x_bf[0], x_raw[0], 0, T)
         nc.vector.tensor_copy(
             out=w4_scales_dealt[:],
-            in_=scale_rows[:, :, :M].rearrange("p g (m r) -> p g r m", r=PACK),
+            in_=w4_scale_rows.rearrange("p g (m r) -> p g r m", r=PACK),
         )
         deal_w4(1)
         quantize_x(0)
-        interleave("vector", x_bf[1], x_raw[1], 0, 320)
-        interleave("scalar", x_bf[1], x_raw[1], 320, T)
+        interleave("scalar", x_bf[1], x_raw[1], 0, T)
+        split_w8((0, 0), 96)
         quantize_x(1)
-        deal_w8("vector", (0, 0), 0, 80)
-        deal_w8("scalar", (0, 0), 80, P)
         quantize_w((0, 0))
-        fp4_passes(0, 0)
-        fp4_passes(0, 1)
-        fp8_passes(0, 0)
+        open_group(0)
 
-        for a in range(GROUPS):
-            last = a == GROUPS - 1
-            deal_w8("vector", (1, a), 0, 88)
-            deal_w8("scalar", (1, a), 88, P)
-            for r in range(PACK):
-                quantize_w_slot((1, a), r)
-            fp8_passes(a, 1)
-            if a > 0:
-                interleave("scalar", res_bf[a - 1], res[a - 1], 320, T)
-                interleave("vector", res_bf[a - 1], res[a - 1], 0, 320)
-                quantize_res(a - 1)
-                store_codes(a - 1)
-            if not last:
-                for r in range(PACK):
-                    gelu(a, r, 0, T)
-                store_res(a, 0, PACK)
-                deal_w8("vector", (0, a + 1), 0, P)
-                quantize_w((0, a + 1))
-                fp4_passes(a + 1, 0)
-                fp4_passes(a + 1, 1)
-                fp8_passes(a + 1, 0)
-            else:
-                gelu(a, 0, 0, T)
-                gelu(a, 1, 0, T)
-                store_res(a, 0, 2)
-                for lo, hi in ((0, T // 2), (T // 2, T)):
-                    gelu(a, 2, lo, hi)
-                    gelu(a, 3, lo, hi)
-                    interleave("vector", res_bf[a], res[a], lo, hi)
-                store_res(a, 2, PACK)
-                quantize_res(a)
-                store_codes(a)
+        finish_group(0, 88)
+        for r in range(PACK):
+            gelu(0, r, 0, T)
+        store_res(0, 0, PACK)
+        deal_w8("vector", (0, 1), 0, P)
+        quantize_w((0, 1))
+        open_group(1)
+
+        interleave("scalar", res_bf[0], res[0], 0, T)
+        finish_group(1, P)
+        for r in range(PACK):
+            gelu(1, r, 0, T)
+        store_res(1, 0, PACK)
+        deal_w8("vector", (0, 2), 0, P)
+        quantize_w((0, 2))
+        open_group(2)
+
+        finish_group(2, 96)
+        interleave("scalar", res_bf[1], res[1], 288, T)
+        interleave("vector", res_bf[1], res[1], 0, 288)
+        quantize_res(0)
+        store_codes(0)
+        gelu(2, 0, 0, T)
+        gelu(2, 1, 0, T)
+        quantize_res(1)
+        store_codes(1)
+        store_res(2, 0, 2)
+        for lo, hi in ((0, T // 2), (T // 2, T)):
+            gelu(2, 2, lo, hi)
+            gelu(2, 3, lo, hi)
+        store_res(2, 2, PACK)
+        interleave("vector", res_bf[2], res[2], 0, T // 2)
+        interleave("vector", res_bf[2], res[2], T // 2, 432)
+        interleave("scalar", res_bf[2], res[2], 432, T)
+        quantize_res(2)
+        store_codes(2)
         for q in range(QUADS):
             nc.scalar.dma_start(
                 out=out_2[:, 4 * q : 4 * q + 4, :].rearrange("a r t -> r a t").bitcast(I32),

@@ -169,11 +169,6 @@ def tile_mix_atom_fm_pl_gelu_kernel(
                 quantize_w_slot((1, a), r)
             fp8_passes(a, 1)
 
-        def open_group(a):
-            fp4_passes(a, 0)
-            fp4_passes(a, 1)
-            fp8_passes(a, 0)
-
         def load_w4(g):
             nc.sync.dma_start(out=w4_raw[g][:].bitcast(I32), in_=w4_words[g].bitcast(I32))
 
@@ -182,39 +177,44 @@ def tile_mix_atom_fm_pl_gelu_kernel(
         nc.gpsimd.dma_start(out=bias[:], in_=b.rearrange("(a p r) -> p a r", p=P, r=PACK))
         nc.scalar.activation(out=warm[:, 1:2], in_=warm[:, 0:1], func=GELU)
         load_w4(0)
-        load_x8(0)
         load_scale_rows(nc.sync, w4_scale_rows, w4_scales)
-        load_w4(1)
-        load_x8(1)
-        load_w8(ga[0])
         nc.sync.dma_start(
             out=x4_codes[:].bitcast(I32), in_=x4_words.rearrange("g p n -> p g n").bitcast(I32)
         )
+        load_w4(1)
+        load_x8(0)
         load_scale_rows(nc.sync, x4_scale_rows, x4_scales)
-        for k in ga[1:]:
+        load_x8(1)
+        for k in ga:
             load_w8(k)
 
         deal_w4(0)
-        interleave("scalar", x_bf[0], x_raw[0], 0, T)
         nc.vector.tensor_copy(
             out=w4_scales_dealt[:],
             in_=w4_scale_rows.rearrange("p g (m r) -> p g r m", r=PACK),
         )
         deal_w4(1)
+        for g in range(PASSES):
+            fp4_passes(0, g)
+            fp4_passes(1, g)
+        interleave("scalar", x_bf[0], x_raw[0], 0, T)
+        interleave("vector", x_bf[1], x_raw[1], 0, 192)
+        interleave("scalar", x_bf[1], x_raw[1], 192, T)
         quantize_x(0)
-        interleave("scalar", x_bf[1], x_raw[1], 0, T)
         split_w8((0, 0), 96)
         quantize_x(1)
         quantize_w((0, 0))
-        open_group(0)
+        fp8_passes(0, 0)
 
         finish_group(0, 88)
         for r in range(PACK):
             gelu(0, r, 0, T)
         store_res(0, 0, PACK)
+        fp4_passes(2, 0)
         deal_w8("vector", (0, 1), 0, P)
         quantize_w((0, 1))
-        open_group(1)
+        fp8_passes(1, 0)
+        fp4_passes(2, 1)
 
         interleave("scalar", res_bf[0], res[0], 0, T)
         finish_group(1, P)
@@ -223,11 +223,11 @@ def tile_mix_atom_fm_pl_gelu_kernel(
         store_res(1, 0, PACK)
         deal_w8("vector", (0, 2), 0, P)
         quantize_w((0, 2))
-        open_group(2)
+        fp8_passes(2, 0)
 
-        finish_group(2, 96)
-        interleave("scalar", res_bf[1], res[1], 288, T)
-        interleave("vector", res_bf[1], res[1], 0, 288)
+        finish_group(2, 112)
+        interleave("scalar", res_bf[1], res[1], 312, T)
+        interleave("vector", res_bf[1], res[1], 0, 312)
         quantize_res(0)
         store_codes(0)
         gelu(2, 0, 0, T)
@@ -240,8 +240,8 @@ def tile_mix_atom_fm_pl_gelu_kernel(
             gelu(2, 3, lo, hi)
         store_res(2, 2, PACK)
         interleave("vector", res_bf[2], res[2], 0, T // 2)
-        interleave("vector", res_bf[2], res[2], T // 2, 432)
-        interleave("scalar", res_bf[2], res[2], 432, T)
+        interleave("vector", res_bf[2], res[2], T // 2, 416)
+        interleave("scalar", res_bf[2], res[2], 416, T)
         quantize_res(2)
         store_codes(2)
         for q in range(QUADS):

@@ -1,9 +1,10 @@
 from contextlib import ExitStack
 
 import concourse.mybir as mybir
+from concourse.masks import make_identity
 
-O, M, T = 1024, 1536, 512
-FLOPS = 2 * 2 * O * M * T
+K_EACH, N_OUT, T = 1024, 1536, 512
+FLOPS = 2 * 2 * K_EACH * N_OUT * T
 
 F32 = mybir.dt.float32
 BF16 = mybir.dt.bfloat16
@@ -17,9 +18,18 @@ GELU = mybir.ActivationFunctionType.Gelu_apprx_tanh
 P = 128
 PACK = 4
 SPAN = P * PACK
-PASSES = O // SPAN
-GROUPS = M // SPAN
-QUADS = 4
+PASSES = K_EACH // SPAN
+GROUPS = N_OUT // SPAN
+FP4_WORD = 2
+QUADRANT = 32
+SCALE_ROWS = 4
+RUN = 4
+HALF = T // 2
+LOW_SLOTS, HIGH_SLOTS = (0, 2), (2, PACK)
+
+X_PASS_1_CUT = 192
+GROUP_1_CUT = 288
+GROUP_2_CUT = 352
 
 
 def tile_mix_atom_fm_pl_gelu_kernel(
@@ -34,48 +44,66 @@ def tile_mix_atom_fm_pl_gelu_kernel(
         def tile(name, shape, dtype):
             return sb.tile(shape, dtype, name=name, align_bytes=64)
 
-        ga = [(g, a) for a in range(GROUPS) for g in range(PASSES)]
+        chunks = [(g, a) for a in range(GROUPS) for g in range(PASSES)]
         x_raw = [tile(f"x_raw{g}", [P, PACK, T], F32) for g in range(PASSES)]
         x_bf = [tile(f"x_bf{g}", [P, T, PACK], BF16) for g in range(PASSES)]
         x_codes = [tile(f"x_codes{g}", [P, T], U32) for g in range(PASSES)]
         x_scales = [tile(f"x_scales{g}", [P, T], U8) for g in range(PASSES)]
-        w_raw = {k: tile(f"w_raw{k[0]}{k[1]}", [P, PACK, SPAN], F32) for k in ga}
-        w_bf = {k: tile(f"w_bf{k[0]}{k[1]}", [P, PACK, P, PACK], BF16) for k in ga}
-        w_codes = {k: tile(f"w_codes{k[0]}{k[1]}", [P, SPAN], U32) for k in ga}
-        w_scales = {k: tile(f"w_scales{k[0]}{k[1]}", [P, SPAN], U8) for k in ga}
-        w4_raw = [tile(f"w4_raw{g}", [P, 2 * M], U8) for g in range(PASSES)]
-        w4_dealt = [tile(f"w4_dealt{g}", [P, PACK, 2 * M // PACK], U8) for g in range(PASSES)]
-        x4_codes = tile("x4_codes", [P, PASSES, 2 * T], U8)
-        scale_rows = tile("scale_rows", [P, PASSES * (M + T)], U8)
-        w4_scale_rows = scale_rows[:, : PASSES * M].rearrange("p (g n) -> p g n", g=PASSES)
-        x4_scale_rows = scale_rows[:, PASSES * M :].rearrange("p (g t) -> p g t", g=PASSES)
-        w4_scales_dealt = tile("w4_scales_dealt", [P, PASSES, PACK, M // PACK], U8)
-        bias = tile("bias", [P, GROUPS, PACK], F32)
-        warm = tile("warm", [P, 2], F32)
+        w_raw = {c: tile(f"w_raw{c[0]}{c[1]}", [P, PACK, SPAN], F32) for c in chunks}
+        w_bf = {c: tile(f"w_bf{c[0]}{c[1]}", [P, PACK, P, PACK], BF16) for c in chunks}
+        w_codes = {c: tile(f"w_codes{c[0]}{c[1]}", [P, SPAN], U32) for c in chunks}
+        w_scales = {c: tile(f"w_scales{c[0]}{c[1]}", [P, SPAN], U8) for c in chunks}
+        w4_raw = [tile(f"w4_raw{g}", [P, FP4_WORD * N_OUT], U8) for g in range(PASSES)]
+        w4_dealt = [tile(f"w4_dealt{g}", [P, PACK, FP4_WORD * N_OUT // PACK], U8) for g in range(PASSES)]
+        x4_codes = tile("x4_codes", [P, PASSES, FP4_WORD * T], U8)
+        scale_rows = tile("scale_rows", [P, PASSES * (N_OUT + T)], U8)
+        w4_scale_rows = scale_rows[:, : PASSES * N_OUT].rearrange("p (g n) -> p g n", g=PASSES)
+        x4_scale_rows = scale_rows[:, PASSES * N_OUT :].rearrange("p (g t) -> p g t", g=PASSES)
+        w4_scales_dealt = tile("w4_scales_dealt", [P, PASSES, PACK, N_OUT // PACK], U8)
+        bias_rows = tile("bias_rows", [P, SPAN], F32)
+        identity = tile("identity", [P, P], F32)
+        bias = tile("bias", [P, PACK, GROUPS], F32)
         res = [tile(f"res{a}", [P, PACK, T], F32) for a in range(GROUPS)]
         res_bf = [tile(f"res_bf{a}", [P, T, PACK], BF16) for a in range(GROUPS)]
-        res_codes = [tile(f"res_codes{a}", [P, T], U32) for a in range(GROUPS)]
+        res_codes = tile("res_codes", [P, GROUPS, T], U32)
         res_scales = tile("res_scales", [P, GROUPS, T], U8)
         acc = {}
 
-        def copy_on(engine, out, in_):
-            if engine == "vector":
-                nc.vector.tensor_copy(out=out, in_=in_)
-            else:
-                nc.scalar.copy(out=out, in_=in_)
+        def load_x8(g):
+            rows = x8[g * SPAN : (g + 1) * SPAN, :]
+            nc.sync.dma_start(out=x_raw[g][:], in_=rows.rearrange("(p j) t -> p j t", j=PACK))
 
-        def interleave(engine, dst, src, lo, hi):
-            copy_on(
-                engine,
-                dst[:, lo:hi, :].rearrange("p (c i) j -> p c j i", i=4),
-                src[:, :, lo:hi].rearrange("p j (c i) -> p c j i", i=4),
+        def load_w8(g, a):
+            rows = w8[g * SPAN : (g + 1) * SPAN, a * SPAN : (a + 1) * SPAN]
+            nc.sync.dma_start(out=w_raw[g, a][:], in_=rows.rearrange("(p j) n -> p j n", j=PACK))
+
+        def load_w4(g):
+            nc.sync.dma_start(out=w4_raw[g][:].bitcast(I32), in_=w4_words[g].bitcast(I32))
+
+        def load_scale_rows(target, source):
+            for i in range(SCALE_ROWS):
+                nc.sync.dma_start(
+                    out=target[i:P:QUADRANT, :, :].bitcast(I32),
+                    in_=source[:, i : SPAN // 32 : SCALE_ROWS, :].rearrange("g q n -> q g n").bitcast(I32),
+                )
+
+        def interleave(cast, dst, src, lo, hi):
+            cast(
+                out=dst[:, lo:hi, :].rearrange("p (c i) j -> p c j i", i=RUN),
+                in_=src[:, :, lo:hi].rearrange("p j (c i) -> p c j i", i=RUN),
             )
 
-        def deal_w8(engine, k, lo, hi):
-            copy_on(
-                engine,
-                w_bf[k][:, :, lo:hi, :].rearrange("p r m j -> p m r j"),
-                w_raw[k][:, :, PACK * lo : PACK * hi].rearrange("p j (m r) -> p m r j", r=PACK),
+        def deal_w8(cast, chunk, slots):
+            lo, hi = slots
+            cast(
+                out=w_bf[chunk][:, lo:hi, :, :].rearrange("p r m j -> p m j r"),
+                in_=w_raw[chunk][:].rearrange("p j (m r) -> p m j r", r=PACK)[:, :, :, lo:hi],
+            )
+
+        def deal_w4(g):
+            nc.vector.tensor_copy(
+                out=w4_dealt[g][:].rearrange("p r (m e) -> p r m e", e=FP4_WORD),
+                in_=w4_raw[g][:].rearrange("p (m r e) -> p r m e", r=PACK, e=FP4_WORD),
             )
 
         def quantize(codes, scales, values):
@@ -84,26 +112,21 @@ def tile_mix_atom_fm_pl_gelu_kernel(
         def quantize_x(g):
             quantize(x_codes[g][:], x_scales[g][:], x_bf[g][:].rearrange("p t j -> p (t j)"))
 
-        def quantize_w(k):
-            quantize(w_codes[k][:], w_scales[k][:], w_bf[k][:].rearrange("p r m j -> p (r m j)"))
+        def quantize_w(chunk, slots):
+            lo, hi = slots
+            cols = slice(lo * P, hi * P)
+            values = w_bf[chunk][:, lo:hi, :, :].rearrange("p r m j -> p (r m j)")
+            quantize(w_codes[chunk][:, cols], w_scales[chunk][:, cols], values)
 
-        def quantize_w_slot(k, r):
-            cols = slice(r * P, (r + 1) * P)
-            quantize(w_codes[k][:, cols], w_scales[k][:, cols], w_bf[k][:, r, :, :].rearrange("p m j -> p (m j)"))
+        def quantize_res(a, lo, hi):
+            values = res_bf[a][:, lo:hi, :].rearrange("p t r -> p (t r)")
+            quantize(res_codes[:, a, lo:hi], res_scales[:, a, lo:hi], values)
 
-        def quantize_res(a):
-            quantize(res_codes[a][:], res_scales[:, a, :], res_bf[a][:].rearrange("p t r -> p (t r)"))
-
-        def deal_w4(g):
-            nc.vector.tensor_copy(
-                out=w4_dealt[g][:].rearrange("p r (m e) -> p r m e", e=2),
-                in_=w4_raw[g][:].rearrange("p (m r e) -> p r m e", r=PACK, e=2),
-            )
-
-        def load_w8(k):
-            g, a = k
-            rows = w8[g * SPAN : (g + 1) * SPAN, a * SPAN : (a + 1) * SPAN]
-            nc.sync.dma_start(out=w_raw[k][:], in_=rows.rearrange("(p j) n -> p j n", j=PACK))
+        def prepare_w8(chunk):
+            deal_w8(nc.vector.tensor_copy, chunk, LOW_SLOTS)
+            deal_w8(nc.vector.tensor_copy, chunk, HIGH_SLOTS)
+            quantize_w(chunk, LOW_SLOTS)
+            quantize_w(chunk, HIGH_SLOTS)
 
         def fp4_passes(a, g):
             for r in range(PACK):
@@ -111,7 +134,7 @@ def tile_mix_atom_fm_pl_gelu_kernel(
                     acc[a, r] = psum.tile([P, T], F32, name=f"acc{r}")
                 nc.tensor.matmul_mx(
                     out=acc[a, r][:],
-                    lhsT=w4_dealt[g][:, r, 2 * P * a : 2 * P * (a + 1)].bitcast(FP4X4),
+                    lhsT=w4_dealt[g][:, r, FP4_WORD * P * a : FP4_WORD * P * (a + 1)].bitcast(FP4X4),
                     lhsT_scale=w4_scales_dealt[:, g, r, P * a : P * (a + 1)],
                     rhs=x4_codes[:, g, :].bitcast(FP4X4),
                     rhs_scale=x4_scale_rows[:, g, :],
@@ -134,118 +157,110 @@ def tile_mix_atom_fm_pl_gelu_kernel(
 
         def gelu(a, r, lo, hi):
             nc.scalar.activation(
-                out=res[a][:, r, lo:hi], in_=acc[a, r][:, lo:hi], func=GELU, bias=bias[:, a, r : r + 1]
+                out=res[a][:, r, lo:hi], in_=acc[a, r][:, lo:hi], func=GELU, bias=bias[:, r, a : a + 1]
             )
 
-        def store_res(a, lo, hi):
+        def store_res(a, slots):
+            lo, hi = slots
             rows = out_0[a * SPAN : (a + 1) * SPAN, :].rearrange("(p r) t -> p r t", r=PACK)
             nc.sync.dma_start(out=rows[:, lo:hi, :], in_=res[a][:, lo:hi, :])
 
         def store_codes(a):
             nc.sync.dma_start(
-                out=out_1[a].rearrange("p t i -> p (t i)").bitcast(I32), in_=res_codes[a][:].bitcast(I32)
+                out=out_1[a : a + 1].rearrange("a p t i -> p a (t i)").bitcast(I32),
+                in_=res_codes[:, a : a + 1, :].bitcast(I32),
             )
 
-        def load_scale_rows(queue, plane, source):
-            for r in range(4):
-                queue.dma_start(
-                    out=plane[r:P:32, :, :].bitcast(I32),
-                    in_=source[:, r:16:4, :].rearrange("g q n -> q g n").bitcast(I32),
-                )
-
-        def load_x8(g):
-            nc.sync.dma_start(
-                out=x_raw[g][:], in_=x8[g * SPAN : (g + 1) * SPAN, :].rearrange("(p j) t -> p j t", j=PACK)
-            )
-
-        def split_w8(k, cut):
-            deal_w8("vector", k, 0, cut)
-            if cut < P:
-                deal_w8("scalar", k, cut, P)
-
-        def finish_group(a, cut):
-            split_w8((1, a), cut)
-            for r in range(PACK):
-                quantize_w_slot((1, a), r)
-            fp8_passes(a, 1)
-
-        def load_w4(g):
-            nc.sync.dma_start(out=w4_raw[g][:].bitcast(I32), in_=w4_words[g].bitcast(I32))
+        all_slots = (0, PACK)
 
         nc.vector.memset(scale_rows[:].bitcast(I32), 0)
-        nc.gpsimd.memset(warm[:, 0:1], 0.0)
-        nc.gpsimd.dma_start(out=bias[:], in_=b.rearrange("(a p r) -> p a r", p=P, r=PACK))
-        nc.scalar.activation(out=warm[:, 1:2], in_=warm[:, 0:1], func=GELU)
+
+        nc.gpsimd.memset(bias_rows[:], 0.0)
+        nc.scalar.dma_start(out=bias_rows[:GROUPS, :], in_=b.rearrange("(a n) -> a n", a=GROUPS))
+        make_identity(nc, identity[:])
+        bias_turned = psum.tile([P, PACK, P], F32, name="acc0")
+        for r in range(PACK):
+            nc.tensor.transpose(bias_turned[:, r, :], bias_rows[:, r:SPAN:PACK], identity[:])
+        nc.scalar.copy(out=bias[:], in_=bias_turned[:, :, :GROUPS])
+
         load_w4(0)
-        load_scale_rows(nc.sync, w4_scale_rows, w4_scales)
-        nc.sync.dma_start(
-            out=x4_codes[:].bitcast(I32), in_=x4_words.rearrange("g p n -> p g n").bitcast(I32)
-        )
-        load_w4(1)
+        load_scale_rows(w4_scale_rows, w4_scales)
         load_x8(0)
-        load_scale_rows(nc.sync, x4_scale_rows, x4_scales)
+        nc.sync.dma_start(out=x4_codes[:].bitcast(I32), in_=x4_words.rearrange("g p n -> p g n").bitcast(I32))
+        load_w4(1)
+        load_scale_rows(x4_scale_rows, x4_scales)
         load_x8(1)
-        for k in ga:
-            load_w8(k)
+        for g, a in chunks:
+            load_w8(g, a)
 
         deal_w4(0)
         nc.vector.tensor_copy(
-            out=w4_scales_dealt[:],
-            in_=w4_scale_rows.rearrange("p g (m r) -> p g r m", r=PACK),
+            out=w4_scales_dealt[:], in_=w4_scale_rows.rearrange("p g (m r) -> p g r m", r=PACK)
         )
         deal_w4(1)
-        for g in range(PASSES):
-            fp4_passes(0, g)
-            fp4_passes(1, g)
-        interleave("scalar", x_bf[0], x_raw[0], 0, T)
-        interleave("vector", x_bf[1], x_raw[1], 0, 192)
-        interleave("scalar", x_bf[1], x_raw[1], 192, T)
+        fp4_passes(0, 0)
+        fp4_passes(0, 1)
+        fp4_passes(1, 0)
+        interleave(nc.scalar.copy, x_bf[0], x_raw[0], 0, T)
+        interleave(nc.vector.tensor_copy, x_bf[1], x_raw[1], 0, X_PASS_1_CUT)
+        interleave(nc.scalar.copy, x_bf[1], x_raw[1], X_PASS_1_CUT, T)
         quantize_x(0)
-        split_w8((0, 0), 96)
+        deal_w8(nc.vector.tensor_copy, (0, 0), LOW_SLOTS)
+        deal_w8(nc.scalar.copy, (0, 0), HIGH_SLOTS)
         quantize_x(1)
-        quantize_w((0, 0))
+        quantize_w((0, 0), all_slots)
         fp8_passes(0, 0)
 
-        finish_group(0, 88)
+        prepare_w8((1, 0))
+        fp8_passes(0, 1)
         for r in range(PACK):
             gelu(0, r, 0, T)
-        store_res(0, 0, PACK)
-        fp4_passes(2, 0)
-        deal_w8("vector", (0, 1), 0, P)
-        quantize_w((0, 1))
+        store_res(0, all_slots)
+        fp4_passes(1, 1)
+        prepare_w8((0, 1))
         fp8_passes(1, 0)
-        fp4_passes(2, 1)
+        fp4_passes(2, 0)
 
-        interleave("scalar", res_bf[0], res[0], 0, T)
-        finish_group(1, P)
+        interleave(nc.scalar.copy, res_bf[0], res[0], 0, T)
+        prepare_w8((1, 1))
+        fp8_passes(1, 1)
+        fp4_passes(2, 1)
         for r in range(PACK):
             gelu(1, r, 0, T)
-        store_res(1, 0, PACK)
-        deal_w8("vector", (0, 2), 0, P)
-        quantize_w((0, 2))
+        store_res(1, all_slots)
+        deal_w8(nc.vector.tensor_copy, (0, 2), LOW_SLOTS)
+        deal_w8(nc.vector.tensor_copy, (0, 2), HIGH_SLOTS)
+        quantize_res(0, 0, T)
+        quantize_w((0, 2), all_slots)
         fp8_passes(2, 0)
-
-        finish_group(2, 112)
-        interleave("scalar", res_bf[1], res[1], 312, T)
-        interleave("vector", res_bf[1], res[1], 0, 312)
-        quantize_res(0)
         store_codes(0)
+
+        interleave(nc.scalar.copy, res_bf[1], res[1], GROUP_1_CUT, T)
+        for lo, hi in (LOW_SLOTS, HIGH_SLOTS):
+            deal_w8(nc.vector.tensor_copy, (1, 2), (lo, hi))
+            for r in range(lo, hi):
+                quantize_w((1, 2), (r, r + 1))
+        fp8_passes(2, 1)
+        interleave(nc.vector.tensor_copy, res_bf[1], res[1], 0, GROUP_1_CUT)
         gelu(2, 0, 0, T)
         gelu(2, 1, 0, T)
-        quantize_res(1)
+        store_res(2, LOW_SLOTS)
+        quantize_res(1, 0, T)
         store_codes(1)
-        store_res(2, 0, 2)
-        for lo, hi in ((0, T // 2), (T // 2, T)):
-            gelu(2, 2, lo, hi)
-            gelu(2, 3, lo, hi)
-        store_res(2, 2, PACK)
-        interleave("vector", res_bf[2], res[2], 0, T // 2)
-        interleave("vector", res_bf[2], res[2], T // 2, 416)
-        interleave("scalar", res_bf[2], res[2], 416, T)
-        quantize_res(2)
+
+        gelu(2, 2, 0, T)
+        gelu(2, 3, 0, HALF)
+        gelu(2, 3, HALF, T)
+        store_res(2, HIGH_SLOTS)
+        interleave(nc.vector.tensor_copy, res_bf[2], res[2], 0, HALF)
+        interleave(nc.vector.tensor_copy, res_bf[2], res[2], HALF, GROUP_2_CUT)
+        interleave(nc.scalar.copy, res_bf[2], res[2], GROUP_2_CUT, T)
+        quantize_res(2, 0, HALF)
+        quantize_res(2, HALF, T)
         store_codes(2)
-        for q in range(QUADS):
+
+        for q in range(P // QUADRANT):
             nc.scalar.dma_start(
-                out=out_2[:, 4 * q : 4 * q + 4, :].rearrange("a r t -> r a t").bitcast(I32),
-                in_=res_scales[32 * q : 32 * q + 4, :, :].bitcast(I32),
+                out=out_2[:, SCALE_ROWS * q : SCALE_ROWS * (q + 1), :].rearrange("a i t -> i a t").bitcast(I32),
+                in_=res_scales[QUADRANT * q : QUADRANT * q + SCALE_ROWS, :, :].bitcast(I32),
             )

from contextlib import ExitStack

import concourse.mybir as mybir
from concourse.masks import make_identity

K_EACH, N_OUT, T = 1024, 1536, 512
FLOPS = 2 * 2 * K_EACH * N_OUT * T

F32 = mybir.dt.float32
BF16 = mybir.dt.bfloat16
I32 = mybir.dt.int32
U32 = mybir.dt.uint32
U8 = mybir.dt.uint8
FP8X4 = mybir.dt.float8_e4m3fn_x4
FP4X4 = mybir.dt.float4_e2m1fn_x4
GELU = mybir.ActivationFunctionType.Gelu_apprx_tanh

P = 128
PACK = 4
SPAN = P * PACK
PASSES = K_EACH // SPAN
GROUPS = N_OUT // SPAN
FP4_WORD = 2
QUADRANT = 32
SCALE_ROWS = 4
RUN = 4
HALF = T // 2
LOW_SLOTS, HIGH_SLOTS = (0, 2), (2, PACK)

X_PASS_1_CUT = 192
GROUP_1_CUT = 288
GROUP_2_CUT = 352


def tile_mix_atom_fm_pl_gelu_kernel(
    tc, x8, w8, x4_words, x4_scales, w4_words, w4_scales, b, out_0, out_1, out_2
):
    nc = tc.nc
    with ExitStack() as ctx:
        sb = ctx.enter_context(tc.tile_pool(name="sb", bufs=1))
        psum = ctx.enter_context(tc.psum_pool(name="psum", bufs=2))
        ctx.enter_context(tc.manual_schedule())

        def tile(name, shape, dtype):
            return sb.tile(shape, dtype, name=name, align_bytes=64)

        chunks = [(g, a) for a in range(GROUPS) for g in range(PASSES)]
        x_raw = [tile(f"x_raw{g}", [P, PACK, T], F32) for g in range(PASSES)]
        x_bf = [tile(f"x_bf{g}", [P, T, PACK], BF16) for g in range(PASSES)]
        x_codes = [tile(f"x_codes{g}", [P, T], U32) for g in range(PASSES)]
        x_scales = [tile(f"x_scales{g}", [P, T], U8) for g in range(PASSES)]
        w_raw = {c: tile(f"w_raw{c[0]}{c[1]}", [P, PACK, SPAN], F32) for c in chunks}
        w_bf = {c: tile(f"w_bf{c[0]}{c[1]}", [P, PACK, P, PACK], BF16) for c in chunks}
        w_codes = {c: tile(f"w_codes{c[0]}{c[1]}", [P, SPAN], U32) for c in chunks}
        w_scales = {c: tile(f"w_scales{c[0]}{c[1]}", [P, SPAN], U8) for c in chunks}
        w4_raw = [tile(f"w4_raw{g}", [P, FP4_WORD * N_OUT], U8) for g in range(PASSES)]
        w4_dealt = [tile(f"w4_dealt{g}", [P, PACK, FP4_WORD * N_OUT // PACK], U8) for g in range(PASSES)]
        x4_codes = tile("x4_codes", [P, PASSES, FP4_WORD * T], U8)
        scale_rows = tile("scale_rows", [P, PASSES * (N_OUT + T)], U8)
        w4_scale_rows = scale_rows[:, : PASSES * N_OUT].rearrange("p (g n) -> p g n", g=PASSES)
        x4_scale_rows = scale_rows[:, PASSES * N_OUT :].rearrange("p (g t) -> p g t", g=PASSES)
        w4_scales_dealt = tile("w4_scales_dealt", [P, PASSES, PACK, N_OUT // PACK], U8)
        bias_rows = tile("bias_rows", [P, SPAN], F32)
        identity = tile("identity", [P, P], F32)
        bias = tile("bias", [P, PACK, GROUPS], F32)
        res = [tile(f"res{a}", [P, PACK, T], F32) for a in range(GROUPS)]
        res_bf = [tile(f"res_bf{a}", [P, T, PACK], BF16) for a in range(GROUPS)]
        res_codes = tile("res_codes", [P, GROUPS, T], U32)
        res_scales = tile("res_scales", [P, GROUPS, T], U8)
        acc = {}

        def load_x8(g):
            rows = x8[g * SPAN : (g + 1) * SPAN, :]
            nc.sync.dma_start(out=x_raw[g][:], in_=rows.rearrange("(p j) t -> p j t", j=PACK))

        def load_w8(g, a):
            rows = w8[g * SPAN : (g + 1) * SPAN, a * SPAN : (a + 1) * SPAN]
            nc.sync.dma_start(out=w_raw[g, a][:], in_=rows.rearrange("(p j) n -> p j n", j=PACK))

        def load_w4(g):
            nc.sync.dma_start(out=w4_raw[g][:].bitcast(I32), in_=w4_words[g].bitcast(I32))

        def load_scale_rows(target, source):
            for i in range(SCALE_ROWS):
                nc.sync.dma_start(
                    out=target[i:P:QUADRANT, :, :].bitcast(I32),
                    in_=source[:, i : SPAN // 32 : SCALE_ROWS, :].rearrange("g q n -> q g n").bitcast(I32),
                )

        def interleave(cast, dst, src, lo, hi):
            cast(
                out=dst[:, lo:hi, :].rearrange("p (c i) j -> p c j i", i=RUN),
                in_=src[:, :, lo:hi].rearrange("p j (c i) -> p c j i", i=RUN),
            )

        def deal_w8(cast, chunk, slots):
            lo, hi = slots
            cast(
                out=w_bf[chunk][:, lo:hi, :, :].rearrange("p r m j -> p m j r"),
                in_=w_raw[chunk][:].rearrange("p j (m r) -> p m j r", r=PACK)[:, :, :, lo:hi],
            )

        def deal_w4(g):
            nc.vector.tensor_copy(
                out=w4_dealt[g][:].rearrange("p r (m e) -> p r m e", e=FP4_WORD),
                in_=w4_raw[g][:].rearrange("p (m r e) -> p r m e", r=PACK, e=FP4_WORD),
            )

        def quantize(codes, scales, values):
            nc.vector.quantize_mx(out=codes.bitcast(FP8X4), scales=scales, in_=values)

        def quantize_x(g):
            quantize(x_codes[g][:], x_scales[g][:], x_bf[g][:].rearrange("p t j -> p (t j)"))

        def quantize_w(chunk, slots):
            lo, hi = slots
            cols = slice(lo * P, hi * P)
            values = w_bf[chunk][:, lo:hi, :, :].rearrange("p r m j -> p (r m j)")
            quantize(w_codes[chunk][:, cols], w_scales[chunk][:, cols], values)

        def quantize_res(a, lo, hi):
            values = res_bf[a][:, lo:hi, :].rearrange("p t r -> p (t r)")
            quantize(res_codes[:, a, lo:hi], res_scales[:, a, lo:hi], values)

        def prepare_w8(chunk):
            deal_w8(nc.vector.tensor_copy, chunk, LOW_SLOTS)
            deal_w8(nc.vector.tensor_copy, chunk, HIGH_SLOTS)
            quantize_w(chunk, LOW_SLOTS)
            quantize_w(chunk, HIGH_SLOTS)

        def fp4_passes(a, g):
            for r in range(PACK):
                if g == 0:
                    acc[a, r] = psum.tile([P, T], F32, name=f"acc{r}")
                nc.tensor.matmul_mx(
                    out=acc[a, r][:],
                    lhsT=w4_dealt[g][:, r, FP4_WORD * P * a : FP4_WORD * P * (a + 1)].bitcast(FP4X4),
                    lhsT_scale=w4_scales_dealt[:, g, r, P * a : P * (a + 1)],
                    rhs=x4_codes[:, g, :].bitcast(FP4X4),
                    rhs_scale=x4_scale_rows[:, g, :],
                    start=(g == 0),
                    stop=False,
                )

        def fp8_passes(a, g):
            for r in range(PACK):
                cols = slice(r * P, (r + 1) * P)
                nc.tensor.matmul_mx(
                    out=acc[a, r][:],
                    lhsT=w_codes[g, a][:, cols].bitcast(FP8X4),
                    lhsT_scale=w_scales[g, a][:, cols],
                    rhs=x_codes[g][:].bitcast(FP8X4),
                    rhs_scale=x_scales[g][:],
                    start=False,
                    stop=(g == PASSES - 1),
                )

        def gelu(a, r, lo, hi):
            nc.scalar.activation(
                out=res[a][:, r, lo:hi], in_=acc[a, r][:, lo:hi], func=GELU, bias=bias[:, r, a : a + 1]
            )

        def store_res(a, slots):
            lo, hi = slots
            rows = out_0[a * SPAN : (a + 1) * SPAN, :].rearrange("(p r) t -> p r t", r=PACK)
            nc.sync.dma_start(out=rows[:, lo:hi, :], in_=res[a][:, lo:hi, :])

        def store_codes(a):
            nc.sync.dma_start(
                out=out_1[a : a + 1].rearrange("a p t i -> p a (t i)").bitcast(I32),
                in_=res_codes[:, a : a + 1, :].bitcast(I32),
            )

        all_slots = (0, PACK)

        nc.vector.memset(scale_rows[:].bitcast(I32), 0)

        nc.gpsimd.memset(bias_rows[:], 0.0)
        nc.scalar.dma_start(out=bias_rows[:GROUPS, :], in_=b.rearrange("(a n) -> a n", a=GROUPS))
        make_identity(nc, identity[:])
        bias_turned = psum.tile([P, PACK, P], F32, name="acc0")
        for r in range(PACK):
            nc.tensor.transpose(bias_turned[:, r, :], bias_rows[:, r:SPAN:PACK], identity[:])
        nc.scalar.copy(out=bias[:], in_=bias_turned[:, :, :GROUPS])

        load_w4(0)
        load_scale_rows(w4_scale_rows, w4_scales)
        load_x8(0)
        nc.sync.dma_start(out=x4_codes[:].bitcast(I32), in_=x4_words.rearrange("g p n -> p g n").bitcast(I32))
        load_w4(1)
        load_scale_rows(x4_scale_rows, x4_scales)
        load_x8(1)
        for g, a in chunks:
            load_w8(g, a)

        deal_w4(0)
        nc.vector.tensor_copy(
            out=w4_scales_dealt[:], in_=w4_scale_rows.rearrange("p g (m r) -> p g r m", r=PACK)
        )
        deal_w4(1)
        fp4_passes(0, 0)
        fp4_passes(0, 1)
        fp4_passes(1, 0)
        interleave(nc.scalar.copy, x_bf[0], x_raw[0], 0, T)
        interleave(nc.vector.tensor_copy, x_bf[1], x_raw[1], 0, X_PASS_1_CUT)
        interleave(nc.scalar.copy, x_bf[1], x_raw[1], X_PASS_1_CUT, T)
        quantize_x(0)
        deal_w8(nc.vector.tensor_copy, (0, 0), LOW_SLOTS)
        deal_w8(nc.scalar.copy, (0, 0), HIGH_SLOTS)
        quantize_x(1)
        quantize_w((0, 0), all_slots)
        fp8_passes(0, 0)

        prepare_w8((1, 0))
        fp8_passes(0, 1)
        for r in range(PACK):
            gelu(0, r, 0, T)
        store_res(0, all_slots)
        fp4_passes(1, 1)
        prepare_w8((0, 1))
        fp8_passes(1, 0)
        fp4_passes(2, 0)

        interleave(nc.scalar.copy, res_bf[0], res[0], 0, T)
        prepare_w8((1, 1))
        fp8_passes(1, 1)
        fp4_passes(2, 1)
        for r in range(PACK):
            gelu(1, r, 0, T)
        store_res(1, all_slots)
        deal_w8(nc.vector.tensor_copy, (0, 2), LOW_SLOTS)
        deal_w8(nc.vector.tensor_copy, (0, 2), HIGH_SLOTS)
        quantize_res(0, 0, T)
        quantize_w((0, 2), all_slots)
        fp8_passes(2, 0)
        store_codes(0)

        interleave(nc.scalar.copy, res_bf[1], res[1], GROUP_1_CUT, T)
        for lo, hi in (LOW_SLOTS, HIGH_SLOTS):
            deal_w8(nc.vector.tensor_copy, (1, 2), (lo, hi))
            for r in range(lo, hi):
                quantize_w((1, 2), (r, r + 1))
        fp8_passes(2, 1)
        interleave(nc.vector.tensor_copy, res_bf[1], res[1], 0, GROUP_1_CUT)
        gelu(2, 0, 0, T)
        gelu(2, 1, 0, T)
        store_res(2, LOW_SLOTS)
        quantize_res(1, 0, T)
        store_codes(1)

        gelu(2, 2, 0, T)
        gelu(2, 3, 0, HALF)
        gelu(2, 3, HALF, T)
        store_res(2, HIGH_SLOTS)
        interleave(nc.vector.tensor_copy, res_bf[2], res[2], 0, HALF)
        interleave(nc.vector.tensor_copy, res_bf[2], res[2], HALF, GROUP_2_CUT)
        interleave(nc.scalar.copy, res_bf[2], res[2], GROUP_2_CUT, T)
        quantize_res(2, 0, HALF)
        quantize_res(2, HALF, T)
        store_codes(2)

        for q in range(P // QUADRANT):
            nc.scalar.dma_start(
                out=out_2[:, SCALE_ROWS * q : SCALE_ROWS * (q + 1), :].rearrange("a i t -> i a t").bitcast(I32),
                in_=res_scales[QUADRANT * q : QUADRANT * q + SCALE_ROWS, :, :].bitcast(I32),
            )
